import numpy as np
import ml_dtypes


def mxq(x, axis, fmt="e4m3"):
    dtype, down = {"e4m3": (ml_dtypes.float8_e4m3fn, 7), "e5m2": (ml_dtypes.float8_e5m2, 14)}[fmt]
    v = np.moveaxis(np.asarray(x, np.float32).astype(ml_dtypes.bfloat16).astype(np.float64), axis, -1)
    blocks = v.reshape(v.shape[:-1] + (-1, 32))
    amax = np.abs(blocks).max(-1, keepdims=True)
    byte = np.maximum(np.where(amax > 0, np.frexp(amax)[1] - 1 + 127, 0) - down, 1)
    scale = np.exp2(byte - 127.0)
    codes = (blocks / scale).astype(np.float32).astype(dtype).astype(np.float64)
    return np.moveaxis((codes * scale).reshape(v.shape), -1, axis)


WIDE = False


def mx_kscale(k):
    if not WIDE:
        return np.ones(k)
    levels = np.array([10, -10, 5, -5, 0])
    if k % 512:
        return np.exp2(np.random.permutation(np.resize(levels, k // 32))).repeat(32)
    a = np.empty((k // 512, 16))
    for p in range(k // 512):
        a[p, :8] = np.random.permutation(np.resize(levels, 8))
        for g in range(8):
            far = levels[np.abs(levels - a[p, g]) >= 10]
            a[p, g + 8] = far[np.random.randint(len(far))]
    return np.exp2(a.ravel()).repeat(32)


def f64(x):
    return np.asarray(x).astype(np.float64)


def striped(idx):
    return np.tile(idx.reshape(-1, 16).T, (8, 1)).astype(np.uint16)


def unstriped(offs):
    return offs[:16].T.reshape(-1).astype(np.int64)


E2M1 = np.array([0.0, 0.5, 1.0, 1.5, 2.0, 3.0, 4.0, 6.0, -0.0, -0.5, -1.0, -1.5, -2.0, -3.0, -4.0, -6.0])


def pack_weight(w, fmt):
    k, n = w.shape
    w = f64(np.asarray(w, np.float32).astype(ml_dtypes.bfloat16)).reshape(k // 32, 32, n)
    amax = np.abs(w).max(1)
    if fmt == "e4m3":
        byte = np.frexp(amax)[1] - 1 + 127 - 7
    else:
        mant, ex = np.frexp(amax / 6.0)
        byte = np.where(mant > 0.5, ex, ex - 1) + 127
    byte = np.clip(np.where(amax > 0, byte, 1), 1, 254)
    scaled = (w * np.exp2(127.0 - byte)[:, None, :]).reshape(k, n).astype(np.float32)
    by_word = np.ascontiguousarray(scaled.reshape(k // 512, 128, 4, n).transpose(0, 1, 3, 2))
    if fmt == "e4m3":
        words = by_word.astype(ml_dtypes.float8_e4m3fn).view(np.uint8)
    else:
        c = by_word.astype(ml_dtypes.float4_e2m1fn).view(np.uint8) & 0xF
        words = (c[..., 0::2] | (c[..., 1::2] << 4)).reshape(k // 512, 128, 2 * n)
    return np.ascontiguousarray(words), np.ascontiguousarray(byte.astype(np.uint8).reshape(k // 512, 16, n))


def unpack_weight(words, scales, fmt):
    g, _, n = scales.shape
    words = np.ascontiguousarray(words).reshape(g, 128, n, -1)
    if fmt == "e4m3":
        vals = words.view(ml_dtypes.float8_e4m3fn).astype(np.float64)
    else:
        nib = np.empty((g, 128, n, 4), np.uint8)
        nib[..., 0::2] = words & 0xF
        nib[..., 1::2] = words >> 4
        vals = E2M1[nib]
    vals = vals * np.repeat(np.exp2(scales.astype(np.float64) - 127.0), 8, axis=1)[..., None]
    return vals.transpose(0, 1, 3, 2).reshape(g * 512, n)


def gelu(v):
    return 0.5 * v * (1.0 + np.tanh(np.sqrt(2.0 / np.pi) * (v + 0.044715 * v**3)))


def bf(x):
    return np.asarray(x, np.float32).astype(ml_dtypes.bfloat16)

def planes(Y):
    n, m = Y.shape
    b = f64(bf(Y)).reshape(n // 32, 32, m)
    amax = np.abs(b).max(1)
    byte = np.clip(np.where(amax > 0, np.frexp(amax)[1] - 1 + 127 - 7, 1), 1, 254)
    codes = (b * np.exp2(127.0 - byte)[:, None, :]).reshape(n, m).astype(np.float32).astype(ml_dtypes.float8_e4m3fn).view(np.uint8)
    words = codes.reshape(n // 512, 128, 4, m).transpose(0, 1, 3, 2)
    return np.ascontiguousarray(words), np.ascontiguousarray(byte.astype(np.uint8).reshape(n // 512, 16, m))


K, T, S, H, T2, S2 = 1024, 2048, 512, 1024, 4096, 1024

def setup_inputs():
    n = np.random.standard_normal
    s = mx_kscale(K)[:, None]
    u = mx_kscale(H)[:, None]
    r = np.sqrt(u)
    idx = np.random.permutation(T)[:S]
    idx2 = np.random.permutation(T2)[:S2]
    tab_words, tab_scales = pack_weight(n((K, T)) * s, "e4m3")
    w4_words, w4_scales = pack_weight(0.8 * n((K, H)) / np.sqrt(K) / s * r.T, "e2m1")
    w1 = 0.6 * n((K, H)) / np.sqrt(K) / s * r.T
    knee = 1.5 * np.exp(0.2 * n(H)) * r[:, 0]
    size = np.exp(0.8 * n(T2))
    tab2_words, tab2_scales = pack_weight(0.12 * n((H, T2)) / np.sqrt(H) / u * size, "e4m3")
    top = size[idx2]
    bias = (0.5 + 0.1 * n(S2)) * top
    return {"tab_words": tab_words, "tab_scales": tab_scales, "offs": striped(idx),
            "w4_words": w4_words, "w4_scales": w4_scales, "w1": w1.astype(np.float32),
            "knee": knee.astype(np.float32), "roof": (2.0 * knee).astype(np.float32),
            "tab2_words": tab2_words, "tab2_scales": tab2_scales, "offs2": striped(idx2),
            "bias": bias.astype(np.float32), "top": top.astype(np.float32)}

def reference(tab_words, tab_scales, offs, w4_words, w4_scales, w1, knee, roof,
              tab2_words, tab2_scales, offs2, bias, top):
    v = unpack_weight(tab_words, tab_scales, "e4m3")[:, unstriped(offs)]
    v2 = unpack_weight(tab2_words, tab2_scales, "e4m3")[:, unstriped(offs2)]
    w4 = unpack_weight(w4_words, w4_scales, "e2m1")
    p = w4.T @ v + mxq(f64(w1), 0, "e4m3").T @ v
    h = p * np.clip(p + f64(knee)[:, None], 0.0, f64(roof)[:, None])
    d = v2.T @ mxq(h, 0, "e4m3")
    y = np.clip(d + f64(bias)[:, None], 0.0, f64(top)[:, None])
    words, scales = planes(y)
    return y, words, scales

@@ -1,0 +1,278 @@
+from contextlib import ExitStack
+
+import concourse.mybir as mybir
+
+K, T, S, H, T2, S2 = 1024, 2048, 512, 1024, 4096, 1024
+FLOPS = 2 * (2 * K * H * S + H * S2 * S)
+
+F32 = mybir.dt.float32
+BF16 = mybir.dt.bfloat16
+I32 = mybir.dt.int32
+U32 = mybir.dt.uint32
+U16 = mybir.dt.uint16
+U8 = mybir.dt.uint8
+FP8X4 = mybir.dt.float8_e4m3fn_x4
+FP4X4 = mybir.dt.float4_e2m1fn_x4
+ALU = mybir.AluOpType
+ACT = mybir.ActivationFunctionType
+
+P = 128
+PACK = 4
+PASS = P * PACK
+QUADS = 4
+U_ROW = 4
+
+
+def tile_list_crop_attribute_strengths_kernel(
+    tc, tab_words, tab_scales, offs, w4_words, w4_scales, w1, knee, roof,
+    tab2_words, tab2_scales, offs2, bias, top, out_0, out_1, out_2,
+):
+    nc = tc.nc
+    with ExitStack() as ctx:
+        keep = ctx.enter_context(tc.tile_pool(name="keep", bufs=1))
+        stage = ctx.enter_context(tc.tile_pool(name="stage", bufs=4))
+        work = ctx.enter_context(tc.tile_pool(name="work", bufs=2))
+        psum = ctx.enter_context(tc.psum_pool(name="psum", bufs=8))
+
+        def kept(shape, dtype, name):
+            return keep.tile(shape, dtype, name=name, align_bytes=64)
+
+        list1 = keep.tile([P, S // 16], U16, name="list1")
+        list2 = keep.tile([P, S2 // 16], U16, name="list2")
+
+        tab_sc = kept([P, 2 * T], U8, "tab_sc")
+        w4_sc_raw = kept([P, 2 * H], U8, "w4_sc_raw")
+        tab2_sc = kept([P, T2], U8, "tab2_sc")
+        nc.vector.memset(tab_sc[:].bitcast(I32), 0)
+        nc.vector.memset(w4_sc_raw[:].bitcast(I32), 0)
+        nc.vector.memset(tab2_sc[:].bitcast(I32), 0)
+
+        def load_side_by_side(dst, src, q):
+            nc.sync.dma_start(
+                out=dst[32 * q : 32 * q + 4, :].bitcast(I32).rearrange("r (a n) -> r a n", a=2),
+                in_=src[:, 4 * q : 4 * q + 4, :].bitcast(I32).rearrange("a r n -> r a n"),
+            )
+
+        def load_w1(g, b):
+            raw = stage.tile([P, PACK, PASS], F32, name="w1_raw", tag="stage", align_bytes=64)
+            rows = w1[g * PASS : (g + 1) * PASS, b * PASS : (b + 1) * PASS]
+            nc.sync.dma_start(out=raw[:], in_=rows.rearrange("(p j) n -> p j n", j=PACK))
+            return raw
+
+        def load_words(table, a, width):
+            words = stage.tile([P, width], I32, name="words", tag="stage", align_bytes=64)
+            nc.sync.dma_start(out=words[:], in_=table[a].rearrange("p n i -> p (n i)").bitcast(I32))
+            return words
+
+        def load_channels(vec, name):
+            cols = keep.tile([P, 2, 8], F32, name=name)
+            nc.gpsimd.dma_start(out=cols[:, :, 0:PACK], in_=vec.rearrange("(b p t) -> p b t", b=2, t=PACK))
+            return cols
+
+        knee_c = load_channels(knee, "knee_c")
+        roof_c = load_channels(roof, "roof_c")
+        bias_c = load_channels(bias, "bias_c")
+        top_c = load_channels(top, "top_c")
+
+        w1_raw = {}
+        tab_w = [load_words(tab_words, 0, T)]
+        nc.sync.dma_start(list1[:], offs)
+        for q in range(QUADS):
+            load_side_by_side(tab_sc, tab_scales, q)
+        w4_raw = kept([P, 2 * 2 * H], U8, "w4_raw")
+        nc.sync.dma_start(
+            out=w4_raw[:].bitcast(I32).rearrange("p (a n) -> p a n", a=2),
+            in_=w4_words.bitcast(I32).rearrange("a p n -> p a n"),
+        )
+        load_side_by_side(w4_sc_raw, w4_scales, 0)
+        tab_w.append(load_words(tab_words, 1, T))
+        for q in range(1, QUADS):
+            load_side_by_side(w4_sc_raw, w4_scales, q)
+        w1_raw[0, 0] = load_w1(0, 0)
+        nc.sync.dma_start(list2[:], offs2)
+        for q in range(QUADS):
+            nc.sync.dma_start(
+                out=tab2_sc[32 * q + U_ROW : 32 * q + U_ROW + 8, :].bitcast(I32),
+                in_=tab2_scales[:, 4 * q : 4 * q + 4, :].bitcast(I32),
+            )
+        w1_raw[1, 0] = load_w1(1, 0)
+        w1_raw[0, 1] = load_w1(0, 1)
+        w1_raw[1, 1] = load_w1(1, 1)
+        tab2_w = [load_words(tab2_words, a, T2) for a in range(2)]
+
+        w1_codes, w1_sc = {}, {}
+
+        def quantise_w1(g, b, vector_from):
+            grouped = keep.tile([P, PACK, P, PACK], BF16, name="w1_grouped", tag=f"w1_grouped{g}{b}", align_bytes=64)
+            dst = grouped[:].rearrange("p t m j -> p m t j")
+            src = w1_raw[g, b][:].rearrange("p j (m t) -> p m t j", t=PACK)
+            if vector_from > 0:
+                nc.scalar.copy(out=dst[:, 0:vector_from], in_=src[:, 0:vector_from])
+            if vector_from < P:
+                nc.vector.tensor_copy(out=dst[:, vector_from:P], in_=src[:, vector_from:P])
+            w1_codes[g, b] = kept([P, PASS], U32, f"w1_codes{g}{b}")
+            w1_sc[g, b] = kept([P, PASS], U8, f"w1_sc{g}{b}")
+            nc.vector.quantize_mx(
+                out=w1_codes[g, b][:].bitcast(FP8X4), scales=w1_sc[g, b][:],
+                in_=grouped[:].rearrange("p t m j -> p (t m j)"),
+            )
+
+        v_codes = [kept([P, S], U32, f"v_codes{a}") for a in range(2)]
+        v_sc = [kept([P, S], U8, f"v_sc{a}") for a in range(2)]
+        nc.vector.tensor_copy(out=v_codes[0][:], in_=tab_w[0][:].bitcast(U32).indirect(list1[:]))
+        for a in range(2):
+            nc.vector.tensor_copy(out=v_sc[a][:], in_=tab_sc[:, a * T : (a + 1) * T].indirect(list1[:]))
+
+        nc.vector.tensor_copy(out=v_codes[1][:], in_=tab_w[1][:].bitcast(U32).indirect(list1[:]))
+
+        w4_codes, w4_sc = [], []
+
+        def deal_w4(b):
+            w4_sc.append(kept([P, 2, PASS], U8, f"w4_sc{b}"))
+            nc.vector.tensor_copy(
+                out=w4_sc[b][:].rearrange("p g (t m) -> p g t m", t=PACK),
+                in_=w4_sc_raw[:].rearrange("p (g b m t) -> p b g t m", g=2, b=2, t=PACK)[:, b],
+            )
+            w4_codes.append(kept([P, 2, 2 * PASS], U8, f"w4_codes{b}"))
+            nc.scalar.copy(
+                out=w4_codes[b][:].bitcast(U16).rearrange("p g (t m) -> p g t m", t=PACK),
+                in_=w4_raw[:].bitcast(U16).rearrange("p (g b m t) -> p b g t m", g=2, b=2, t=PACK)[:, b],
+            )
+
+        deal_w4(0)
+        deal_w4(1)
+        u_sc_flat = kept([P, S2], U8, "u_sc_flat")
+        nc.vector.tensor_copy(out=u_sc_flat[:], in_=tab2_sc[:].indirect(list2[:]))
+        quantise_w1(0, 0, 128)
+        quantise_w1(1, 0, 64)
+
+        def interleave(dst, src):
+            return dict(
+                out=dst[:].rearrange("p (c i) t -> p c t i", i=4),
+                in_=src[:].rearrange("p t (c i) -> p c t i", i=4),
+            )
+
+        def w4_pass(acc, g, b, t, start, stop):
+            nc.tensor.matmul_mx(
+                out=acc[:], lhsT=w4_codes[b][:, g, 2 * t * P : 2 * (t + 1) * P].bitcast(FP4X4),
+                lhsT_scale=w4_sc[b][:, g, t * P : (t + 1) * P],
+                rhs=v_codes[g][:].bitcast(FP8X4), rhs_scale=v_sc[g][:], start=start, stop=stop,
+            )
+
+        def w1_pass(acc, g, b, t, start, stop):
+            nc.tensor.matmul_mx(
+                out=acc[:], lhsT=w1_codes[g, b][:, t * P : (t + 1) * P].bitcast(FP8X4),
+                lhsT_scale=w1_sc[g, b][:, t * P : (t + 1) * P],
+                rhs=v_codes[g][:].bitcast(FP8X4), rhs_scale=v_sc[g][:], start=start, stop=stop,
+            )
+
+        h_codes, h_sc = [], []
+
+        def swish(acc, flat, b, t):
+            gate = keep.tile([P, S], F32, name="gate", tag=f"gate{b}{t}", align_bytes=64)
+            nc.scalar.activation(out=gate[:], in_=acc[:], func=ACT.Relu, bias=knee_c[:, b, t : t + 1])
+            nc.vector.scalar_tensor_tensor(
+                out=flat[:, t, :], in0=gate[:], scalar=roof_c[:, b, t : t + 1], in1=acc[:],
+                op0=ALU.min, op1=ALU.mult,
+            )
+
+        def quantise_h(flat, b, copy):
+            grouped = keep.tile([P, S, PACK], BF16, name="h_grouped", tag=f"h_grouped{b}", align_bytes=64)
+            copy(**interleave(grouped, flat))
+            h_codes.append(kept([P, S], U32, f"h_codes{b}"))
+            h_sc.append(kept([P, S], U8, f"h_sc{b}"))
+            nc.vector.quantize_mx(
+                out=h_codes[b][:].bitcast(FP8X4), scales=h_sc[b][:],
+                in_=grouped[:].rearrange("p c t -> p (c t)"),
+            )
+
+        u_codes = {}
+
+        def gather_tab2(a, g, tag):
+            u_codes[a, g] = keep.tile([P, PASS], U32, name="u_codes", tag=tag, align_bytes=64)
+            nc.vector.tensor_copy(
+                out=u_codes[a, g][:].rearrange("p (t m) -> p m t", t=PACK),
+                in_=tab2_w[a][:].bitcast(U32).indirect(list2[:, 32 * g : 32 * (g + 1)]),
+            )
+
+        accs = [psum.tile([P, S], F32, name="acc", tag="acc") for t in range(PACK)]
+        for t in range(PACK):
+            for g in range(2):
+                w4_pass(accs[t], g, 0, t, g == 0, False)
+        for t in range(PACK):
+            w1_pass(accs[t], 0, 0, t, False, False)
+        quantise_w1(0, 1, 64)
+        quantise_w1(1, 1, 64)
+        flat0 = work.tile([P, PACK, S], BF16, name="h_flat", align_bytes=64)
+        for t in range(PACK):
+            w1_pass(accs[t], 1, 0, t, False, True)
+            swish(accs[t], flat0, 0, t)
+
+        accs = [psum.tile([P, S], F32, name="acc", tag="acc") for t in range(PACK)]
+        for t in range(PACK):
+            for g in range(2):
+                w4_pass(accs[t], g, 1, t, g == 0, False)
+        for t in range(PACK):
+            w1_pass(accs[t], 0, 1, t, False, False)
+        flat1 = work.tile([P, PACK, S], BF16, name="h_flat", align_bytes=64)
+        for t in range(PACK):
+            w1_pass(accs[t], 1, 1, t, False, True)
+            swish(accs[t], flat1, 1, t)
+        quantise_h(flat0, 0, nc.scalar.copy)
+        quantise_h(flat1, 1, nc.scalar.copy)
+        u_sc = keep.tile([P, S2], U8, name="u_sc", tag="w1_grouped10", align_bytes=64)
+        nc.vector.tensor_copy(
+            out=u_sc[:].rearrange("p (g t m) -> p g t m", g=2, t=PACK),
+            in_=u_sc_flat[:].rearrange("p (g m t) -> p g t m", g=2, t=PACK),
+        )
+        gather_tab2(0, 0, "gate11")
+        gather_tab2(0, 1, "gate13")
+        gather_tab2(1, 0, "h_grouped0")
+        gather_tab2(1, 1, "h_grouped1")
+
+        def strength_pass(acc, a, g, t):
+            col = g * PASS + t * P
+            nc.tensor.matmul_mx(
+                out=acc[:], lhsT=u_codes[a, g][:, t * P : (t + 1) * P].bitcast(FP8X4),
+                lhsT_scale=u_sc[U_ROW + 4 * a : P, col : col + P],
+                rhs=h_codes[a][:].bitcast(FP8X4), rhs_scale=h_sc[a][:],
+                start=(a == 0), stop=(a == 1),
+            )
+
+        y_sc = kept([P, 2, S], U8, "y_sc")
+        out_rows = out_0.rearrange("(g p t) j -> g p t j", g=2, t=PACK)
+        for g in range(2):
+            accs = [psum.tile([P, S], F32, name="acc", tag="acc") for t in range(PACK)]
+            for t in range(PACK):
+                strength_pass(accs[t], 0, g, t)
+            y = work.tile([P, PACK, S], F32, name="y", align_bytes=64)
+            for t in range(PACK):
+                strength_pass(accs[t], 1, g, t)
+                above = work.tile([P, S], F32, name="above", bufs=3)
+                nc.scalar.activation(out=above[:], in_=accs[t][:], func=ACT.Relu, bias=bias_c[:, g, t : t + 1])
+                nc.vector.tensor_scalar(
+                    out=y[:, t, :], in0=above[:], scalar1=top_c[:, g, t : t + 1], scalar2=None, op0=ALU.min,
+                )
+                nc.sync.dma_start(out=out_rows[g, :, t, :], in_=y[:, t, :])
+            width = S // (g + 1)
+            pieces = [slice(c, c + width) for c in range(0, S, width)]
+            grouped = work.tile([P, S, PACK], BF16, name="y_grouped", align_bytes=64)
+            for cols in pieces:
+                nc.vector.tensor_copy(
+                    out=grouped[:, cols, :].rearrange("p (c i) t -> p c t i", i=4),
+                    in_=y[:, :, cols].rearrange("p t (c i) -> p c t i", i=4),
+                )
+            y_codes = kept([P, S], I32, f"y_codes{g}")
+            for cols in pieces:
+                nc.vector.quantize_mx(
+                    out=y_codes[:, cols].bitcast(FP8X4), scales=y_sc[:, g, cols],
+                    in_=grouped[:, cols, :].rearrange("p c t -> p (c t)"),
+                )
+                nc.sync.dma_start(
+                    out=out_1[g].rearrange("p m t -> p (m t)").bitcast(I32)[:, cols], in_=y_codes[:, cols],
+                )
+        for q in range(QUADS):
+            nc.scalar.dma_start(
+                out=out_2[:, 4 * q : 4 * q + 4, :].bitcast(I32).rearrange("g r n -> r g n"),
+                in_=y_sc[32 * q : 32 * q + 4, :, :].bitcast(I32),
+            )

@@ -30,7 +30,7 @@ def tile_list_crop_attribute_strengths_kernel(
     nc = tc.nc
     with ExitStack() as ctx:
         keep = ctx.enter_context(tc.tile_pool(name="keep", bufs=1))
-        stage = ctx.enter_context(tc.tile_pool(name="stage", bufs=4))
+        stage = ctx.enter_context(tc.tile_pool(name="stage", bufs=5))
         work = ctx.enter_context(tc.tile_pool(name="work", bufs=2))
         psum = ctx.enter_context(tc.psum_pool(name="psum", bufs=8))
 
@@ -43,9 +43,9 @@ def tile_list_crop_attribute_strengths_kernel(
         tab_sc = kept([P, 2 * T], U8, "tab_sc")
         w4_sc_raw = kept([P, 2 * H], U8, "w4_sc_raw")
         tab2_sc = kept([P, T2], U8, "tab2_sc")
+        nc.vector.memset(tab2_sc[:].bitcast(I32), 0)
         nc.vector.memset(tab_sc[:].bitcast(I32), 0)
         nc.vector.memset(w4_sc_raw[:].bitcast(I32), 0)
-        nc.vector.memset(tab2_sc[:].bitcast(I32), 0)
 
         def load_side_by_side(dst, src, q):
             nc.sync.dma_start(
@@ -66,46 +66,44 @@ def tile_list_crop_attribute_strengths_kernel(
 
         def load_channels(vec, name):
             cols = keep.tile([P, 2, 8], F32, name=name)
-            nc.gpsimd.dma_start(out=cols[:, :, 0:PACK], in_=vec.rearrange("(b p t) -> p b t", b=2, t=PACK))
+            nc.sync.dma_start(out=cols[:, :, 0:PACK], in_=vec.rearrange("(b p t) -> p b t", b=2, t=PACK))
             return cols
 
-        knee_c = load_channels(knee, "knee_c")
-        roof_c = load_channels(roof, "roof_c")
-        bias_c = load_channels(bias, "bias_c")
-        top_c = load_channels(top, "top_c")
-
+        for q in range(QUADS):
+            nc.gpsimd.dma_start(
+                out=tab2_sc[32 * q + U_ROW : 32 * q + U_ROW + 8, :].bitcast(I32),
+                in_=tab2_scales[:, 4 * q : 4 * q + 4, :].bitcast(I32),
+            )
         w1_raw = {}
         tab_w = [load_words(tab_words, 0, T)]
         nc.sync.dma_start(list1[:], offs)
         for q in range(QUADS):
             load_side_by_side(tab_sc, tab_scales, q)
+        nc.sync.dma_start(list2[:], offs2)
+        w1_raw[0, 0] = load_w1(0, 0)
         w4_raw = kept([P, 2 * 2 * H], U8, "w4_raw")
         nc.sync.dma_start(
             out=w4_raw[:].bitcast(I32).rearrange("p (a n) -> p a n", a=2),
             in_=w4_words.bitcast(I32).rearrange("a p n -> p a n"),
         )
-        load_side_by_side(w4_sc_raw, w4_scales, 0)
-        tab_w.append(load_words(tab_words, 1, T))
-        for q in range(1, QUADS):
-            load_side_by_side(w4_sc_raw, w4_scales, q)
-        w1_raw[0, 0] = load_w1(0, 0)
-        nc.sync.dma_start(list2[:], offs2)
         for q in range(QUADS):
-            nc.sync.dma_start(
-                out=tab2_sc[32 * q + U_ROW : 32 * q + U_ROW + 8, :].bitcast(I32),
-                in_=tab2_scales[:, 4 * q : 4 * q + 4, :].bitcast(I32),
-            )
+            load_side_by_side(w4_sc_raw, w4_scales, q)
+        tab_w.append(load_words(tab_words, 1, T))
+        knee_c = load_channels(knee, "knee_c")
+        roof_c = load_channels(roof, "roof_c")
         w1_raw[1, 0] = load_w1(1, 0)
         w1_raw[0, 1] = load_w1(0, 1)
         w1_raw[1, 1] = load_w1(1, 1)
+        bias_c = load_channels(bias, "bias_c")
+        top_c = load_channels(top, "top_c")
         tab2_w = [load_words(tab2_words, a, T2) for a in range(2)]
 
         w1_codes, w1_sc = {}, {}
 
         def quantise_w1(g, b, vector_from):
             grouped = keep.tile([P, PACK, P, PACK], BF16, name="w1_grouped", tag=f"w1_grouped{g}{b}", align_bytes=64)
-            dst = grouped[:].rearrange("p t m j -> p m t j")
-            src = w1_raw[g, b][:].rearrange("p j (m t) -> p m t j", t=PACK)
+            dst = grouped[:].rearrange("p t m j -> p m j t")
+            src = w1_raw[g, b][:].rearrange("p j (m t) -> p m j t", t=PACK)
             if vector_from > 0:
                 nc.scalar.copy(out=dst[:, 0:vector_from], in_=src[:, 0:vector_from])
             if vector_from < P:
@@ -123,8 +121,6 @@ def tile_list_crop_attribute_strengths_kernel(
         for a in range(2):
             nc.vector.tensor_copy(out=v_sc[a][:], in_=tab_sc[:, a * T : (a + 1) * T].indirect(list1[:]))
 
-        nc.vector.tensor_copy(out=v_codes[1][:], in_=tab_w[1][:].bitcast(U32).indirect(list1[:]))
-
         w4_codes, w4_sc = [], []
 
         def deal_w4(b):
@@ -139,11 +135,12 @@ def tile_list_crop_attribute_strengths_kernel(
                 in_=w4_raw[:].bitcast(U16).rearrange("p (g b m t) -> p b g t m", g=2, b=2, t=PACK)[:, b],
             )
 
+        quantise_w1(0, 0, 64)
+        u_sc_flat = keep.tile([P, S2], U8, name="u_sc_flat", tag="w1_grouped00", align_bytes=64)
+        nc.vector.tensor_copy(out=u_sc_flat[:], in_=tab2_sc[:].indirect(list2[:]))
         deal_w4(0)
         deal_w4(1)
-        u_sc_flat = kept([P, S2], U8, "u_sc_flat")
-        nc.vector.tensor_copy(out=u_sc_flat[:], in_=tab2_sc[:].indirect(list2[:]))
-        quantise_w1(0, 0, 128)
+        nc.vector.tensor_copy(out=v_codes[1][:], in_=tab_w[1][:].bitcast(U32).indirect(list1[:]))
         quantise_w1(1, 0, 64)
 
         def interleave(dst, src):
@@ -189,18 +186,22 @@ def tile_list_crop_attribute_strengths_kernel(
         u_codes = {}
 
         def gather_tab2(a, g, tag):
-            u_codes[a, g] = keep.tile([P, PASS], U32, name="u_codes", tag=tag, align_bytes=64)
+            picked = keep.tile([P, PASS], U32, name="u_picked", tag=tag, align_bytes=64)
+            nc.vector.tensor_copy(
+                out=picked[:], in_=tab2_w[a][:].bitcast(U32).indirect(list2[:, 32 * g : 32 * (g + 1)]),
+            )
+            u_codes[a, g] = kept([P, PASS], I32, f"u_codes{a}{g}")
             nc.vector.tensor_copy(
                 out=u_codes[a, g][:].rearrange("p (t m) -> p m t", t=PACK),
-                in_=tab2_w[a][:].bitcast(U32).indirect(list2[:, 32 * g : 32 * (g + 1)]),
+                in_=picked[:].bitcast(I32).rearrange("p (m t) -> p m t", t=PACK),
             )
 
         accs = [psum.tile([P, S], F32, name="acc", tag="acc") for t in range(PACK)]
         for t in range(PACK):
-            for g in range(2):
-                w4_pass(accs[t], g, 0, t, g == 0, False)
-        for t in range(PACK):
-            w1_pass(accs[t], 0, 0, t, False, False)
+            w1_pass(accs[t], 0, 0, t, True, False)
+        for g in range(2):
+            for t in range(PACK):
+                w4_pass(accs[t], g, 0, t, False, False)
         quantise_w1(0, 1, 64)
         quantise_w1(1, 1, 64)
         flat0 = work.tile([P, PACK, S], BF16, name="h_flat", align_bytes=64)
@@ -209,8 +210,8 @@ def tile_list_crop_attribute_strengths_kernel(
             swish(accs[t], flat0, 0, t)
 
         accs = [psum.tile([P, S], F32, name="acc", tag="acc") for t in range(PACK)]
-        for t in range(PACK):
-            for g in range(2):
+        for g in range(2):
+            for t in range(PACK):
                 w4_pass(accs[t], g, 1, t, g == 0, False)
         for t in range(PACK):
             w1_pass(accs[t], 0, 1, t, False, False)
@@ -241,36 +242,47 @@ def tile_list_crop_attribute_strengths_kernel(
 
         y_sc = kept([P, 2, S], U8, "y_sc")
         out_rows = out_0.rearrange("(g p t) j -> g p t j", g=2, t=PACK)
+        accs = [psum.tile([P, S], F32, name="acc", tag="acc") for i in range(2 * PACK)]
         for g in range(2):
-            accs = [psum.tile([P, S], F32, name="acc", tag="acc") for t in range(PACK)]
             for t in range(PACK):
-                strength_pass(accs[t], 0, g, t)
-            y = work.tile([P, PACK, S], F32, name="y", align_bytes=64)
+                strength_pass(accs[PACK * g + t], 0, g, t)
+        y, y_grouped = [], []
+
+        def round_y(g, cols, copy):
+            copy(
+                out=y_grouped[g][:, cols, :].rearrange("p (c i) t -> p c t i", i=4),
+                in_=y[g][:, :, cols].rearrange("p t (c i) -> p c t i", i=4),
+            )
+
+        def quantise_y(g, cols, codes):
+            nc.vector.quantize_mx(
+                out=codes[:, cols].bitcast(FP8X4), scales=y_sc[:, g, cols],
+                in_=y_grouped[g][:, cols, :].rearrange("p c t -> p (c t)"),
+            )
+            nc.sync.dma_start(out=out_1[g].rearrange("p m t -> p (m t)").bitcast(I32)[:, cols], in_=codes[:, cols])
+
+        for g in range(2):
+            y.append(work.tile([P, PACK, S], F32, name="y", align_bytes=64))
+            y_grouped.append(work.tile([P, S, PACK], BF16, name="y_grouped", align_bytes=64))
             for t in range(PACK):
-                strength_pass(accs[t], 1, g, t)
-                above = work.tile([P, S], F32, name="above", bufs=3)
-                nc.scalar.activation(out=above[:], in_=accs[t][:], func=ACT.Relu, bias=bias_c[:, g, t : t + 1])
+                strength_pass(accs[PACK * g + t], 1, g, t)
+                above = keep.tile([P, S], F32, name="above", tag=f"above{g}{t}", align_bytes=64)
+                nc.scalar.activation(
+                    out=above[:], in_=accs[PACK * g + t][:], func=ACT.Relu, bias=bias_c[:, g, t : t + 1],
+                )
                 nc.vector.tensor_scalar(
-                    out=y[:, t, :], in0=above[:], scalar1=top_c[:, g, t : t + 1], scalar2=None, op0=ALU.min,
+                    out=y[g][:, t, :], in0=above[:], scalar1=top_c[:, g, t : t + 1], scalar2=None, op0=ALU.min,
                 )
-                nc.sync.dma_start(out=out_rows[g, :, t, :], in_=y[:, t, :])
-            width = S // (g + 1)
-            pieces = [slice(c, c + width) for c in range(0, S, width)]
-            grouped = work.tile([P, S, PACK], BF16, name="y_grouped", align_bytes=64)
-            for cols in pieces:
-                nc.vector.tensor_copy(
-                    out=grouped[:, cols, :].rearrange("p (c i) t -> p c t i", i=4),
-                    in_=y[:, :, cols].rearrange("p t (c i) -> p c t i", i=4),
-                )
-            y_codes = kept([P, S], I32, f"y_codes{g}")
-            for cols in pieces:
-                nc.vector.quantize_mx(
-                    out=y_codes[:, cols].bitcast(FP8X4), scales=y_sc[:, g, cols],
-                    in_=grouped[:, cols, :].rearrange("p c t -> p (c t)"),
-                )
-                nc.sync.dma_start(
-                    out=out_1[g].rearrange("p m t -> p (m t)").bitcast(I32)[:, cols], in_=y_codes[:, cols],
-                )
+                nc.sync.dma_start(out=out_rows[g, :, t, :], in_=y[g][:, t, :])
+            if g == 0:
+                round_y(0, slice(0, S), nc.vector.tensor_copy)
+        left, right = slice(0, S // 2), slice(S // 2, S)
+        round_y(1, left, nc.scalar.copy)
+        round_y(1, right, nc.vector.tensor_copy)
+        quantise_y(0, slice(0, S), keep.tile([P, S], I32, name="y_codes0", tag="above13", align_bytes=64))
+        y_codes1 = kept([P, S], I32, "y_codes1")
+        quantise_y(1, right, y_codes1)
+        quantise_y(1, left, y_codes1)
         for q in range(QUADS):
             nc.scalar.dma_start(
                 out=out_2[:, 4 * q : 4 * q + 4, :].bitcast(I32).rearrange("g r n -> r g n"),

@@ -32,7 +32,7 @@ def tile_list_crop_attribute_strengths_kernel(
         keep = ctx.enter_context(tc.tile_pool(name="keep", bufs=1))
         stage = ctx.enter_context(tc.tile_pool(name="stage", bufs=5))
         work = ctx.enter_context(tc.tile_pool(name="work", bufs=2))
-        psum = ctx.enter_context(tc.psum_pool(name="psum", bufs=8))
+        psum = ctx.enter_context(tc.psum_pool(name="psum", bufs=1))
 
         def kept(shape, dtype, name):
             return keep.tile(shape, dtype, name=name, align_bytes=64)
@@ -64,6 +64,12 @@ def tile_list_crop_attribute_strengths_kernel(
             nc.sync.dma_start(out=words[:], in_=table[a].rearrange("p n i -> p (n i)").bitcast(I32))
             return words
 
+        def load_w4(b):
+            raw = kept([P, 2, 2 * PASS], U8, f"w4_raw{b}")
+            cols = w4_words[:, :, 2 * b * PASS : 2 * (b + 1) * PASS]
+            nc.sync.dma_start(out=raw[:].bitcast(I32), in_=cols.bitcast(I32).rearrange("a p n -> p a n"))
+            return raw
+
         def load_channels(vec, name):
             cols = keep.tile([P, 2, 8], F32, name=name)
             nc.sync.dma_start(out=cols[:, :, 0:PACK], in_=vec.rearrange("(b p t) -> p b t", b=2, t=PACK))
@@ -81,17 +87,14 @@ def tile_list_crop_attribute_strengths_kernel(
             load_side_by_side(tab_sc, tab_scales, q)
         nc.sync.dma_start(list2[:], offs2)
         w1_raw[0, 0] = load_w1(0, 0)
-        w4_raw = kept([P, 2 * 2 * H], U8, "w4_raw")
-        nc.sync.dma_start(
-            out=w4_raw[:].bitcast(I32).rearrange("p (a n) -> p a n", a=2),
-            in_=w4_words.bitcast(I32).rearrange("a p n -> p a n"),
-        )
+        w4_raw = [load_w4(0)]
         for q in range(QUADS):
             load_side_by_side(w4_sc_raw, w4_scales, q)
         tab_w.append(load_words(tab_words, 1, T))
         knee_c = load_channels(knee, "knee_c")
         roof_c = load_channels(roof, "roof_c")
         w1_raw[1, 0] = load_w1(1, 0)
+        w4_raw.append(load_w4(1))
         w1_raw[0, 1] = load_w1(0, 1)
         w1_raw[1, 1] = load_w1(1, 1)
         bias_c = load_channels(bias, "bias_c")
@@ -123,25 +126,29 @@ def tile_list_crop_attribute_strengths_kernel(
 
         w4_codes, w4_sc = [], []
 
-        def deal_w4(b):
+        def deal_w4_scales(b):
             w4_sc.append(kept([P, 2, PASS], U8, f"w4_sc{b}"))
             nc.vector.tensor_copy(
                 out=w4_sc[b][:].rearrange("p g (t m) -> p g t m", t=PACK),
                 in_=w4_sc_raw[:].rearrange("p (g b m t) -> p b g t m", g=2, b=2, t=PACK)[:, b],
             )
+
+        def deal_w4_words(b):
             w4_codes.append(kept([P, 2, 2 * PASS], U8, f"w4_codes{b}"))
             nc.scalar.copy(
                 out=w4_codes[b][:].bitcast(U16).rearrange("p g (t m) -> p g t m", t=PACK),
-                in_=w4_raw[:].bitcast(U16).rearrange("p (g b m t) -> p b g t m", g=2, b=2, t=PACK)[:, b],
+                in_=w4_raw[b][:].bitcast(U16).rearrange("p g (m t) -> p g t m", t=PACK),
             )
 
         quantise_w1(0, 0, 64)
         u_sc_flat = keep.tile([P, S2], U8, name="u_sc_flat", tag="w1_grouped00", align_bytes=64)
         nc.vector.tensor_copy(out=u_sc_flat[:], in_=tab2_sc[:].indirect(list2[:]))
-        deal_w4(0)
-        deal_w4(1)
+        deal_w4_words(0)
+        deal_w4_scales(0)
+        deal_w4_scales(1)
         nc.vector.tensor_copy(out=v_codes[1][:], in_=tab_w[1][:].bitcast(U32).indirect(list1[:]))
         quantise_w1(1, 0, 64)
+        deal_w4_words(1)
 
         def interleave(dst, src):
             return dict(
@@ -196,20 +203,20 @@ def tile_list_crop_attribute_strengths_kernel(
                 in_=picked[:].bitcast(I32).rearrange("p (m t) -> p m t", t=PACK),
             )
 
-        accs = [psum.tile([P, S], F32, name="acc", tag="acc") for t in range(PACK)]
+        accs = [psum.tile([P, S], F32, name="acc", tag=f"bank{t}") for t in range(PACK)]
         for t in range(PACK):
             w1_pass(accs[t], 0, 0, t, True, False)
         for g in range(2):
             for t in range(PACK):
                 w4_pass(accs[t], g, 0, t, False, False)
-        quantise_w1(0, 1, 64)
+        quantise_w1(0, 1, 0)
         quantise_w1(1, 1, 64)
         flat0 = work.tile([P, PACK, S], BF16, name="h_flat", align_bytes=64)
         for t in range(PACK):
             w1_pass(accs[t], 1, 0, t, False, True)
             swish(accs[t], flat0, 0, t)
 
-        accs = [psum.tile([P, S], F32, name="acc", tag="acc") for t in range(PACK)]
+        accs = [psum.tile([P, S], F32, name="acc", tag=f"bank{PACK + t}") for t in range(PACK)]
         for g in range(2):
             for t in range(PACK):
                 w4_pass(accs[t], g, 1, t, g == 0, False)
@@ -227,7 +234,7 @@ def tile_list_crop_attribute_strengths_kernel(
             in_=u_sc_flat[:].rearrange("p (g m t) -> p g t m", g=2, t=PACK),
         )
         gather_tab2(0, 0, "gate11")
-        gather_tab2(0, 1, "gate13")
+        gather_tab2(0, 1, "gate12")
         gather_tab2(1, 0, "h_grouped0")
         gather_tab2(1, 1, "h_grouped1")
 
@@ -242,10 +249,9 @@ def tile_list_crop_attribute_strengths_kernel(
 
         y_sc = kept([P, 2, S], U8, "y_sc")
         out_rows = out_0.rearrange("(g p t) j -> g p t j", g=2, t=PACK)
-        accs = [psum.tile([P, S], F32, name="acc", tag="acc") for i in range(2 * PACK)]
-        for g in range(2):
-            for t in range(PACK):
-                strength_pass(accs[PACK * g + t], 0, g, t)
+        accs = [psum.tile([P, S], F32, name="acc", tag=f"bank{t}") for t in range(PACK)]
+        for t in range(PACK):
+            strength_pass(accs[t], 0, 0, t)
         y, y_grouped = [], []
 
         def round_y(g, cols, copy):
@@ -265,21 +271,24 @@ def tile_list_crop_attribute_strengths_kernel(
             y.append(work.tile([P, PACK, S], F32, name="y", align_bytes=64))
             y_grouped.append(work.tile([P, S, PACK], BF16, name="y_grouped", align_bytes=64))
             for t in range(PACK):
-                strength_pass(accs[PACK * g + t], 1, g, t)
-                above = keep.tile([P, S], F32, name="above", tag=f"above{g}{t}", align_bytes=64)
+                if g == 1:
+                    accs[t] = psum.tile([P, S], F32, name="acc", tag=f"bank{t}")
+                    strength_pass(accs[t], 0, g, t)
+                strength_pass(accs[t], 1, g, t)
+                above = work.tile([P, S], F32, name="above", bufs=4, align_bytes=64)
                 nc.scalar.activation(
-                    out=above[:], in_=accs[PACK * g + t][:], func=ACT.Relu, bias=bias_c[:, g, t : t + 1],
+                    out=above[:], in_=accs[t][:], func=ACT.Relu, bias=bias_c[:, g, t : t + 1],
                 )
                 nc.vector.tensor_scalar(
                     out=y[g][:, t, :], in0=above[:], scalar1=top_c[:, g, t : t + 1], scalar2=None, op0=ALU.min,
                 )
                 nc.sync.dma_start(out=out_rows[g, :, t, :], in_=y[g][:, t, :])
-            if g == 0:
-                round_y(0, slice(0, S), nc.vector.tensor_copy)
         left, right = slice(0, S // 2), slice(S // 2, S)
+        round_y(0, left, nc.vector.tensor_copy)
+        round_y(0, right, nc.vector.tensor_copy)
         round_y(1, left, nc.scalar.copy)
         round_y(1, right, nc.vector.tensor_copy)
-        quantise_y(0, slice(0, S), keep.tile([P, S], I32, name="y_codes0", tag="above13", align_bytes=64))
+        quantise_y(0, slice(0, S), kept([P, S], I32, "y_codes0"))
         y_codes1 = kept([P, S], I32, "y_codes1")
         quantise_y(1, right, y_codes1)
         quantise_y(1, left, y_codes1)

@@ -91,15 +91,15 @@ def tile_list_crop_attribute_strengths_kernel(
         for q in range(QUADS):
             load_side_by_side(w4_sc_raw, w4_scales, q)
         tab_w.append(load_words(tab_words, 1, T))
+        w1_raw[1, 0] = load_w1(1, 0)
         knee_c = load_channels(knee, "knee_c")
         roof_c = load_channels(roof, "roof_c")
-        w1_raw[1, 0] = load_w1(1, 0)
         w4_raw.append(load_w4(1))
         w1_raw[0, 1] = load_w1(0, 1)
         w1_raw[1, 1] = load_w1(1, 1)
+        tab2_w = [load_words(tab2_words, a, T2) for a in range(2)]
         bias_c = load_channels(bias, "bias_c")
         top_c = load_channels(top, "top_c")
-        tab2_w = [load_words(tab2_words, a, T2) for a in range(2)]
 
         w1_codes, w1_sc = {}, {}
 

@@ -20,7 +20,13 @@ P = 128
 PACK = 4
 PASS = P * PACK
 QUADS = 4
-U_ROW = 4
+QUAD = P // QUADS
+LIST_ROWS = 16
+TAB2_ROW = 4
+STAGE_SLOTS = 5
+SCALAR_SHARE = 64
+RUN = 4
+CHANNEL_PITCH = 8
 
 
 def tile_list_crop_attribute_strengths_kernel(
@@ -30,15 +36,21 @@ def tile_list_crop_attribute_strengths_kernel(
     nc = tc.nc
     with ExitStack() as ctx:
         keep = ctx.enter_context(tc.tile_pool(name="keep", bufs=1))
-        stage = ctx.enter_context(tc.tile_pool(name="stage", bufs=5))
+        stage = ctx.enter_context(tc.tile_pool(name="stage", bufs=STAGE_SLOTS))
         work = ctx.enter_context(tc.tile_pool(name="work", bufs=2))
         psum = ctx.enter_context(tc.psum_pool(name="psum", bufs=1))
 
         def kept(shape, dtype, name):
             return keep.tile(shape, dtype, name=name, align_bytes=64)
 
-        list1 = keep.tile([P, S // 16], U16, name="list1")
-        list2 = keep.tile([P, S2 // 16], U16, name="list2")
+        def in_place_of(tag, shape, dtype, name):
+            return keep.tile(shape, dtype, name=name, tag=tag, align_bytes=64)
+
+        def bank(n):
+            return psum.tile([P, S], F32, name="acc", tag=f"bank{n}")
+
+        list1 = keep.tile([P, S // LIST_ROWS], U16, name="list1")
+        list2 = keep.tile([P, S2 // LIST_ROWS], U16, name="list2")
 
         tab_sc = kept([P, 2 * T], U8, "tab_sc")
         w4_sc_raw = kept([P, 2 * H], U8, "w4_sc_raw")
@@ -47,16 +59,17 @@ def tile_list_crop_attribute_strengths_kernel(
         nc.vector.memset(tab_sc[:].bitcast(I32), 0)
         nc.vector.memset(w4_sc_raw[:].bitcast(I32), 0)
 
-        def load_side_by_side(dst, src, q):
-            nc.sync.dma_start(
-                out=dst[32 * q : 32 * q + 4, :].bitcast(I32).rearrange("r (a n) -> r a n", a=2),
-                in_=src[:, 4 * q : 4 * q + 4, :].bitcast(I32).rearrange("a r n -> r a n"),
-            )
+        def load_scales_side_by_side(dst, src):
+            for q in range(QUADS):
+                nc.sync.dma_start(
+                    out=dst[QUAD * q : QUAD * q + 4, :].bitcast(I32).rearrange("r (a n) -> r a n", a=2),
+                    in_=src[:, 4 * q : 4 * q + 4, :].bitcast(I32).rearrange("a r n -> r a n"),
+                )
 
-        def load_w1(g, b):
+        def load_w1(a, b):
             raw = stage.tile([P, PACK, PASS], F32, name="w1_raw", tag="stage", align_bytes=64)
-            rows = w1[g * PASS : (g + 1) * PASS, b * PASS : (b + 1) * PASS]
-            nc.sync.dma_start(out=raw[:], in_=rows.rearrange("(p j) n -> p j n", j=PACK))
+            rows = w1[a * PASS : (a + 1) * PASS, b * PASS : (b + 1) * PASS]
+            nc.sync.dma_start(out=raw[:], in_=rows.rearrange("(p i) n -> p i n", i=PACK))
             return raw
 
         def load_words(table, a, width):
@@ -71,56 +84,56 @@ def tile_list_crop_attribute_strengths_kernel(
             return raw
 
         def load_channels(vec, name):
-            cols = keep.tile([P, 2, 8], F32, name=name)
+            cols = keep.tile([P, 2, CHANNEL_PITCH], F32, name=name)
             nc.sync.dma_start(out=cols[:, :, 0:PACK], in_=vec.rearrange("(b p t) -> p b t", b=2, t=PACK))
             return cols
 
         for q in range(QUADS):
             nc.gpsimd.dma_start(
-                out=tab2_sc[32 * q + U_ROW : 32 * q + U_ROW + 8, :].bitcast(I32),
+                out=tab2_sc[QUAD * q + TAB2_ROW : QUAD * q + TAB2_ROW + 8, :].bitcast(I32),
                 in_=tab2_scales[:, 4 * q : 4 * q + 4, :].bitcast(I32),
             )
         w1_raw = {}
         tab_w = [load_words(tab_words, 0, T)]
         nc.sync.dma_start(list1[:], offs)
-        for q in range(QUADS):
-            load_side_by_side(tab_sc, tab_scales, q)
+        load_scales_side_by_side(tab_sc, tab_scales)
         nc.sync.dma_start(list2[:], offs2)
         w1_raw[0, 0] = load_w1(0, 0)
         w4_raw = [load_w4(0)]
-        for q in range(QUADS):
-            load_side_by_side(w4_sc_raw, w4_scales, q)
+        load_scales_side_by_side(w4_sc_raw, w4_scales)
         tab_w.append(load_words(tab_words, 1, T))
-        w1_raw[1, 0] = load_w1(1, 0)
         knee_c = load_channels(knee, "knee_c")
         roof_c = load_channels(roof, "roof_c")
+        w1_raw[1, 0] = load_w1(1, 0)
         w4_raw.append(load_w4(1))
         w1_raw[0, 1] = load_w1(0, 1)
         w1_raw[1, 1] = load_w1(1, 1)
-        tab2_w = [load_words(tab2_words, a, T2) for a in range(2)]
         bias_c = load_channels(bias, "bias_c")
         top_c = load_channels(top, "top_c")
+        tab2_w = [load_words(tab2_words, a, T2) for a in range(2)]
 
         w1_codes, w1_sc = {}, {}
 
-        def quantise_w1(g, b, vector_from):
-            grouped = keep.tile([P, PACK, P, PACK], BF16, name="w1_grouped", tag=f"w1_grouped{g}{b}", align_bytes=64)
-            dst = grouped[:].rearrange("p t m j -> p m j t")
-            src = w1_raw[g, b][:].rearrange("p j (m t) -> p m j t", t=PACK)
-            if vector_from > 0:
-                nc.scalar.copy(out=dst[:, 0:vector_from], in_=src[:, 0:vector_from])
-            if vector_from < P:
-                nc.vector.tensor_copy(out=dst[:, vector_from:P], in_=src[:, vector_from:P])
-            w1_codes[g, b] = kept([P, PASS], U32, f"w1_codes{g}{b}")
-            w1_sc[g, b] = kept([P, PASS], U8, f"w1_sc{g}{b}")
+        def quantise_w1(a, b):
+            grouped = in_place_of(f"w1_grouped{a}{b}", [P, PACK, P, PACK], BF16, "w1_grouped")
+            dst = grouped[:].rearrange("p t m i -> p m i t")
+            src = w1_raw[a, b][:].rearrange("p i (m t) -> p m i t", t=PACK)
+            nc.scalar.copy(out=dst[:, 0:SCALAR_SHARE], in_=src[:, 0:SCALAR_SHARE])
+            nc.vector.tensor_copy(out=dst[:, SCALAR_SHARE:P], in_=src[:, SCALAR_SHARE:P])
+            w1_codes[a, b] = kept([P, PASS], U32, f"w1_codes{a}{b}")
+            w1_sc[a, b] = kept([P, PASS], U8, f"w1_sc{a}{b}")
             nc.vector.quantize_mx(
-                out=w1_codes[g, b][:].bitcast(FP8X4), scales=w1_sc[g, b][:],
-                in_=grouped[:].rearrange("p t m j -> p (t m j)"),
+                out=w1_codes[a, b][:].bitcast(FP8X4), scales=w1_sc[a, b][:],
+                in_=grouped[:].rearrange("p t m i -> p (t m i)"),
             )
 
         v_codes = [kept([P, S], U32, f"v_codes{a}") for a in range(2)]
         v_sc = [kept([P, S], U8, f"v_sc{a}") for a in range(2)]
-        nc.vector.tensor_copy(out=v_codes[0][:], in_=tab_w[0][:].bitcast(U32).indirect(list1[:]))
+
+        def gather_tab_words(a):
+            nc.vector.tensor_copy(out=v_codes[a][:], in_=tab_w[a][:].bitcast(U32).indirect(list1[:]))
+
+        gather_tab_words(0)
         for a in range(2):
             nc.vector.tensor_copy(out=v_sc[a][:], in_=tab_sc[:, a * T : (a + 1) * T].indirect(list1[:]))
 
@@ -129,60 +142,60 @@ def tile_list_crop_attribute_strengths_kernel(
         def deal_w4_scales(b):
             w4_sc.append(kept([P, 2, PASS], U8, f"w4_sc{b}"))
             nc.vector.tensor_copy(
-                out=w4_sc[b][:].rearrange("p g (t m) -> p g t m", t=PACK),
-                in_=w4_sc_raw[:].rearrange("p (g b m t) -> p b g t m", g=2, b=2, t=PACK)[:, b],
+                out=w4_sc[b][:].rearrange("p a (t m) -> p a t m", t=PACK),
+                in_=w4_sc_raw[:].rearrange("p (a b m t) -> p b a t m", a=2, b=2, t=PACK)[:, b],
             )
 
         def deal_w4_words(b):
             w4_codes.append(kept([P, 2, 2 * PASS], U8, f"w4_codes{b}"))
             nc.scalar.copy(
-                out=w4_codes[b][:].bitcast(U16).rearrange("p g (t m) -> p g t m", t=PACK),
-                in_=w4_raw[b][:].bitcast(U16).rearrange("p g (m t) -> p g t m", t=PACK),
+                out=w4_codes[b][:].bitcast(U16).rearrange("p a (t m) -> p a t m", t=PACK),
+                in_=w4_raw[b][:].bitcast(U16).rearrange("p a (m t) -> p a t m", t=PACK),
             )
 
-        quantise_w1(0, 0, 64)
-        u_sc_flat = keep.tile([P, S2], U8, name="u_sc_flat", tag="w1_grouped00", align_bytes=64)
+        quantise_w1(0, 0)
+        u_sc_flat = in_place_of("w1_grouped00", [P, S2], U8, "u_sc_flat")
         nc.vector.tensor_copy(out=u_sc_flat[:], in_=tab2_sc[:].indirect(list2[:]))
         deal_w4_words(0)
         deal_w4_scales(0)
         deal_w4_scales(1)
-        nc.vector.tensor_copy(out=v_codes[1][:], in_=tab_w[1][:].bitcast(U32).indirect(list1[:]))
-        quantise_w1(1, 0, 64)
+        gather_tab_words(1)
+        quantise_w1(1, 0)
         deal_w4_words(1)
 
-        def interleave(dst, src):
-            return dict(
-                out=dst[:].rearrange("p (c i) t -> p c t i", i=4),
-                in_=src[:].rearrange("p t (c i) -> p c t i", i=4),
+        def interleave(copy, dst, src):
+            copy(
+                out=dst.rearrange("p (c i) t -> p c t i", i=RUN),
+                in_=src.rearrange("p t (c i) -> p c t i", i=RUN),
             )
 
-        def w4_pass(acc, g, b, t, start, stop):
+        def w4_pass(acc, a, b, t, start):
             nc.tensor.matmul_mx(
-                out=acc[:], lhsT=w4_codes[b][:, g, 2 * t * P : 2 * (t + 1) * P].bitcast(FP4X4),
-                lhsT_scale=w4_sc[b][:, g, t * P : (t + 1) * P],
-                rhs=v_codes[g][:].bitcast(FP8X4), rhs_scale=v_sc[g][:], start=start, stop=stop,
+                out=acc[:], lhsT=w4_codes[b][:, a, 2 * t * P : 2 * (t + 1) * P].bitcast(FP4X4),
+                lhsT_scale=w4_sc[b][:, a, t * P : (t + 1) * P],
+                rhs=v_codes[a][:].bitcast(FP8X4), rhs_scale=v_sc[a][:], start=start, stop=False,
             )
 
-        def w1_pass(acc, g, b, t, start, stop):
+        def w1_pass(acc, a, b, t, start, stop):
             nc.tensor.matmul_mx(
-                out=acc[:], lhsT=w1_codes[g, b][:, t * P : (t + 1) * P].bitcast(FP8X4),
-                lhsT_scale=w1_sc[g, b][:, t * P : (t + 1) * P],
-                rhs=v_codes[g][:].bitcast(FP8X4), rhs_scale=v_sc[g][:], start=start, stop=stop,
+                out=acc[:], lhsT=w1_codes[a, b][:, t * P : (t + 1) * P].bitcast(FP8X4),
+                lhsT_scale=w1_sc[a, b][:, t * P : (t + 1) * P],
+                rhs=v_codes[a][:].bitcast(FP8X4), rhs_scale=v_sc[a][:], start=start, stop=stop,
             )
-
-        h_codes, h_sc = [], []
 
         def swish(acc, flat, b, t):
-            gate = keep.tile([P, S], F32, name="gate", tag=f"gate{b}{t}", align_bytes=64)
+            gate = in_place_of(f"gate{b}{t}", [P, S], F32, "gate")
             nc.scalar.activation(out=gate[:], in_=acc[:], func=ACT.Relu, bias=knee_c[:, b, t : t + 1])
             nc.vector.scalar_tensor_tensor(
                 out=flat[:, t, :], in0=gate[:], scalar=roof_c[:, b, t : t + 1], in1=acc[:],
                 op0=ALU.min, op1=ALU.mult,
             )
 
-        def quantise_h(flat, b, copy):
-            grouped = keep.tile([P, S, PACK], BF16, name="h_grouped", tag=f"h_grouped{b}", align_bytes=64)
-            copy(**interleave(grouped, flat))
+        h_codes, h_sc = [], []
+
+        def quantise_h(flat, b):
+            grouped = in_place_of(f"h_grouped{b}", [P, S, PACK], BF16, "h_grouped")
+            interleave(nc.scalar.copy, grouped[:], flat[:])
             h_codes.append(kept([P, S], U32, f"h_codes{b}"))
             h_sc.append(kept([P, S], U8, f"h_sc{b}"))
             nc.vector.quantize_mx(
@@ -190,104 +203,108 @@ def tile_list_crop_attribute_strengths_kernel(
                 in_=grouped[:].rearrange("p c t -> p (c t)"),
             )
 
-        u_codes = {}
-
-        def gather_tab2(a, g, tag):
-            picked = keep.tile([P, PASS], U32, name="u_picked", tag=tag, align_bytes=64)
-            nc.vector.tensor_copy(
-                out=picked[:], in_=tab2_w[a][:].bitcast(U32).indirect(list2[:, 32 * g : 32 * (g + 1)]),
-            )
-            u_codes[a, g] = kept([P, PASS], I32, f"u_codes{a}{g}")
-            nc.vector.tensor_copy(
-                out=u_codes[a, g][:].rearrange("p (t m) -> p m t", t=PACK),
-                in_=picked[:].bitcast(I32).rearrange("p (m t) -> p m t", t=PACK),
-            )
-
-        accs = [psum.tile([P, S], F32, name="acc", tag=f"bank{t}") for t in range(PACK)]
+        accs = [bank(t) for t in range(PACK)]
         for t in range(PACK):
             w1_pass(accs[t], 0, 0, t, True, False)
-        for g in range(2):
+        for a in range(2):
             for t in range(PACK):
-                w4_pass(accs[t], g, 0, t, False, False)
-        quantise_w1(0, 1, 0)
-        quantise_w1(1, 1, 64)
+                w4_pass(accs[t], a, 0, t, False)
+        quantise_w1(0, 1)
+        quantise_w1(1, 1)
         flat0 = work.tile([P, PACK, S], BF16, name="h_flat", align_bytes=64)
         for t in range(PACK):
             w1_pass(accs[t], 1, 0, t, False, True)
             swish(accs[t], flat0, 0, t)
 
-        accs = [psum.tile([P, S], F32, name="acc", tag=f"bank{PACK + t}") for t in range(PACK)]
-        for g in range(2):
+        accs = [bank(PACK + t) for t in range(PACK)]
+        for a in range(2):
             for t in range(PACK):
-                w4_pass(accs[t], g, 1, t, g == 0, False)
+                w4_pass(accs[t], a, 1, t, a == 0)
         for t in range(PACK):
             w1_pass(accs[t], 0, 1, t, False, False)
         flat1 = work.tile([P, PACK, S], BF16, name="h_flat", align_bytes=64)
         for t in range(PACK):
             w1_pass(accs[t], 1, 1, t, False, True)
             swish(accs[t], flat1, 1, t)
-        quantise_h(flat0, 0, nc.scalar.copy)
-        quantise_h(flat1, 1, nc.scalar.copy)
-        u_sc = keep.tile([P, S2], U8, name="u_sc", tag="w1_grouped10", align_bytes=64)
+        quantise_h(flat0, 0)
+        quantise_h(flat1, 1)
+
+        u_sc = in_place_of("w1_grouped10", [P, S2], U8, "u_sc")
         nc.vector.tensor_copy(
             out=u_sc[:].rearrange("p (g t m) -> p g t m", g=2, t=PACK),
             in_=u_sc_flat[:].rearrange("p (g m t) -> p g t m", g=2, t=PACK),
         )
-        gather_tab2(0, 0, "gate11")
-        gather_tab2(0, 1, "gate12")
-        gather_tab2(1, 0, "h_grouped0")
-        gather_tab2(1, 1, "h_grouped1")
+
+        u_codes = {}
+
+        def gather_tab2_words(a, g, tag):
+            u_codes[a, g] = in_place_of(tag, [P, PASS], U32, "u_codes")
+            entries = list2[:, g * PASS // LIST_ROWS : (g + 1) * PASS // LIST_ROWS]
+            nc.vector.tensor_copy(
+                out=u_codes[a, g][:].rearrange("p (t m) -> p m t", t=PACK),
+                in_=tab2_w[a][:].bitcast(U32).indirect(entries),
+            )
+
+        gather_tab2_words(0, 0, "gate11")
+        gather_tab2_words(0, 1, "gate12")
+        gather_tab2_words(1, 0, "h_grouped0")
+        gather_tab2_words(1, 1, "h_grouped1")
 
         def strength_pass(acc, a, g, t):
             col = g * PASS + t * P
             nc.tensor.matmul_mx(
                 out=acc[:], lhsT=u_codes[a, g][:, t * P : (t + 1) * P].bitcast(FP8X4),
-                lhsT_scale=u_sc[U_ROW + 4 * a : P, col : col + P],
+                lhsT_scale=u_sc[TAB2_ROW + 4 * a : P, col : col + P],
                 rhs=h_codes[a][:].bitcast(FP8X4), rhs_scale=h_sc[a][:],
                 start=(a == 0), stop=(a == 1),
             )
 
         y_sc = kept([P, 2, S], U8, "y_sc")
         out_rows = out_0.rearrange("(g p t) j -> g p t j", g=2, t=PACK)
-        accs = [psum.tile([P, S], F32, name="acc", tag=f"bank{t}") for t in range(PACK)]
-        for t in range(PACK):
-            strength_pass(accs[t], 0, 0, t)
         y, y_grouped = [], []
 
-        def round_y(g, cols, copy):
-            copy(
-                out=y_grouped[g][:, cols, :].rearrange("p (c i) t -> p c t i", i=4),
-                in_=y[g][:, :, cols].rearrange("p t (c i) -> p c t i", i=4),
+        def strengths(acc, g, t):
+            strength_pass(acc, 1, g, t)
+            above = work.tile([P, S], F32, name="above", bufs=PACK, align_bytes=64)
+            nc.scalar.activation(out=above[:], in_=acc[:], func=ACT.Relu, bias=bias_c[:, g, t : t + 1])
+            nc.vector.tensor_scalar(
+                out=y[g][:, t, :], in0=above[:], scalar1=top_c[:, g, t : t + 1], scalar2=None, op0=ALU.min,
             )
+            if t % 2 == 1:
+                nc.sync.dma_start(out=out_rows[g, :, t - 1 : t + 1, :], in_=y[g][:, t - 1 : t + 1, :])
+
+        def new_y():
+            y.append(work.tile([P, PACK, S], F32, name="y", align_bytes=64))
+            y_grouped.append(work.tile([P, S, PACK], BF16, name="y_grouped", align_bytes=64))
+
+        accs = [bank(t) for t in range(PACK)]
+        for t in range(PACK):
+            strength_pass(accs[t], 0, 0, t)
+        new_y()
+        for t in range(PACK):
+            strengths(accs[t], 0, t)
+        new_y()
+        for t in range(PACK):
+            acc = bank(t)
+            strength_pass(acc, 0, 1, t)
+            strengths(acc, 1, t)
+
+        def round_y(copy, g, cols):
+            interleave(copy, y_grouped[g][:, cols, :], y[g][:, :, cols])
 
         def quantise_y(g, cols, codes):
             nc.vector.quantize_mx(
                 out=codes[:, cols].bitcast(FP8X4), scales=y_sc[:, g, cols],
                 in_=y_grouped[g][:, cols, :].rearrange("p c t -> p (c t)"),
             )
-            nc.sync.dma_start(out=out_1[g].rearrange("p m t -> p (m t)").bitcast(I32)[:, cols], in_=codes[:, cols])
+            words = out_1[g].rearrange("p m t -> p (m t)").bitcast(I32)
+            nc.sync.dma_start(out=words[:, cols], in_=codes[:, cols])
 
-        for g in range(2):
-            y.append(work.tile([P, PACK, S], F32, name="y", align_bytes=64))
-            y_grouped.append(work.tile([P, S, PACK], BF16, name="y_grouped", align_bytes=64))
-            for t in range(PACK):
-                if g == 1:
-                    accs[t] = psum.tile([P, S], F32, name="acc", tag=f"bank{t}")
-                    strength_pass(accs[t], 0, g, t)
-                strength_pass(accs[t], 1, g, t)
-                above = work.tile([P, S], F32, name="above", bufs=4, align_bytes=64)
-                nc.scalar.activation(
-                    out=above[:], in_=accs[t][:], func=ACT.Relu, bias=bias_c[:, g, t : t + 1],
-                )
-                nc.vector.tensor_scalar(
-                    out=y[g][:, t, :], in0=above[:], scalar1=top_c[:, g, t : t + 1], scalar2=None, op0=ALU.min,
-                )
-                nc.sync.dma_start(out=out_rows[g, :, t, :], in_=y[g][:, t, :])
         left, right = slice(0, S // 2), slice(S // 2, S)
-        round_y(0, left, nc.vector.tensor_copy)
-        round_y(0, right, nc.vector.tensor_copy)
-        round_y(1, left, nc.scalar.copy)
-        round_y(1, right, nc.vector.tensor_copy)
+        round_y(nc.vector.tensor_copy, 0, left)
+        round_y(nc.vector.tensor_copy, 0, right)
+        round_y(nc.scalar.copy, 1, left)
+        round_y(nc.vector.tensor_copy, 1, right)
         quantise_y(0, slice(0, S), kept([P, S], I32, "y_codes0"))
         y_codes1 = kept([P, S], I32, "y_codes1")
         quantise_y(1, right, y_codes1)
@@ -295,5 +312,5 @@ def tile_list_crop_attribute_strengths_kernel(
         for q in range(QUADS):
             nc.scalar.dma_start(
                 out=out_2[:, 4 * q : 4 * q + 4, :].bitcast(I32).rearrange("g r n -> r g n"),
-                in_=y_sc[32 * q : 32 * q + 4, :, :].bitcast(I32),
+                in_=y_sc[QUAD * q : QUAD * q + 4, :, :].bitcast(I32),
             )

from contextlib import ExitStack

import concourse.mybir as mybir

K, T, S, H, T2, S2 = 1024, 2048, 512, 1024, 4096, 1024
FLOPS = 2 * (2 * K * H * S + H * S2 * S)

F32 = mybir.dt.float32
BF16 = mybir.dt.bfloat16
I32 = mybir.dt.int32
U32 = mybir.dt.uint32
U16 = mybir.dt.uint16
U8 = mybir.dt.uint8
FP8X4 = mybir.dt.float8_e4m3fn_x4
FP4X4 = mybir.dt.float4_e2m1fn_x4
ALU = mybir.AluOpType
ACT = mybir.ActivationFunctionType

P = 128
PACK = 4
PASS = P * PACK
QUADS = 4
QUAD = P // QUADS
LIST_ROWS = 16
TAB2_ROW = 4
STAGE_SLOTS = 5
SCALAR_SHARE = 64
RUN = 4
CHANNEL_PITCH = 8


def tile_list_crop_attribute_strengths_kernel(
    tc, tab_words, tab_scales, offs, w4_words, w4_scales, w1, knee, roof,
    tab2_words, tab2_scales, offs2, bias, top, out_0, out_1, out_2,
):
    nc = tc.nc
    with ExitStack() as ctx:
        keep = ctx.enter_context(tc.tile_pool(name="keep", bufs=1))
        stage = ctx.enter_context(tc.tile_pool(name="stage", bufs=STAGE_SLOTS))
        work = ctx.enter_context(tc.tile_pool(name="work", bufs=2))
        psum = ctx.enter_context(tc.psum_pool(name="psum", bufs=1))

        def kept(shape, dtype, name):
            return keep.tile(shape, dtype, name=name, align_bytes=64)

        def in_place_of(tag, shape, dtype, name):
            return keep.tile(shape, dtype, name=name, tag=tag, align_bytes=64)

        def bank(n):
            return psum.tile([P, S], F32, name="acc", tag=f"bank{n}")

        list1 = keep.tile([P, S // LIST_ROWS], U16, name="list1")
        list2 = keep.tile([P, S2 // LIST_ROWS], U16, name="list2")

        tab_sc = kept([P, 2 * T], U8, "tab_sc")
        w4_sc_raw = kept([P, 2 * H], U8, "w4_sc_raw")
        tab2_sc = kept([P, T2], U8, "tab2_sc")
        nc.vector.memset(tab2_sc[:].bitcast(I32), 0)
        nc.vector.memset(tab_sc[:].bitcast(I32), 0)
        nc.vector.memset(w4_sc_raw[:].bitcast(I32), 0)

        def load_scales_side_by_side(dst, src):
            for q in range(QUADS):
                nc.sync.dma_start(
                    out=dst[QUAD * q : QUAD * q + 4, :].bitcast(I32).rearrange("r (a n) -> r a n", a=2),
                    in_=src[:, 4 * q : 4 * q + 4, :].bitcast(I32).rearrange("a r n -> r a n"),
                )

        def load_w1(a, b):
            raw = stage.tile([P, PACK, PASS], F32, name="w1_raw", tag="stage", align_bytes=64)
            rows = w1[a * PASS : (a + 1) * PASS, b * PASS : (b + 1) * PASS]
            nc.sync.dma_start(out=raw[:], in_=rows.rearrange("(p i) n -> p i n", i=PACK))
            return raw

        def load_words(table, a, width):
            words = stage.tile([P, width], I32, name="words", tag="stage", align_bytes=64)
            nc.sync.dma_start(out=words[:], in_=table[a].rearrange("p n i -> p (n i)").bitcast(I32))
            return words

        def load_w4(b):
            raw = kept([P, 2, 2 * PASS], U8, f"w4_raw{b}")
            cols = w4_words[:, :, 2 * b * PASS : 2 * (b + 1) * PASS]
            nc.sync.dma_start(out=raw[:].bitcast(I32), in_=cols.bitcast(I32).rearrange("a p n -> p a n"))
            return raw

        def load_channels(vec, name):
            cols = keep.tile([P, 2, CHANNEL_PITCH], F32, name=name)
            nc.sync.dma_start(out=cols[:, :, 0:PACK], in_=vec.rearrange("(b p t) -> p b t", b=2, t=PACK))
            return cols

        for q in range(QUADS):
            nc.gpsimd.dma_start(
                out=tab2_sc[QUAD * q + TAB2_ROW : QUAD * q + TAB2_ROW + 8, :].bitcast(I32),
                in_=tab2_scales[:, 4 * q : 4 * q + 4, :].bitcast(I32),
            )
        w1_raw = {}
        tab_w = [load_words(tab_words, 0, T)]
        nc.sync.dma_start(list1[:], offs)
        load_scales_side_by_side(tab_sc, tab_scales)
        nc.sync.dma_start(list2[:], offs2)
        w1_raw[0, 0] = load_w1(0, 0)
        w4_raw = [load_w4(0)]
        load_scales_side_by_side(w4_sc_raw, w4_scales)
        tab_w.append(load_words(tab_words, 1, T))
        knee_c = load_channels(knee, "knee_c")
        roof_c = load_channels(roof, "roof_c")
        w1_raw[1, 0] = load_w1(1, 0)
        w4_raw.append(load_w4(1))
        w1_raw[0, 1] = load_w1(0, 1)
        w1_raw[1, 1] = load_w1(1, 1)
        bias_c = load_channels(bias, "bias_c")
        top_c = load_channels(top, "top_c")
        tab2_w = [load_words(tab2_words, a, T2) for a in range(2)]

        w1_codes, w1_sc = {}, {}

        def quantise_w1(a, b):
            grouped = in_place_of(f"w1_grouped{a}{b}", [P, PACK, P, PACK], BF16, "w1_grouped")
            dst = grouped[:].rearrange("p t m i -> p m i t")
            src = w1_raw[a, b][:].rearrange("p i (m t) -> p m i t", t=PACK)
            nc.scalar.copy(out=dst[:, 0:SCALAR_SHARE], in_=src[:, 0:SCALAR_SHARE])
            nc.vector.tensor_copy(out=dst[:, SCALAR_SHARE:P], in_=src[:, SCALAR_SHARE:P])
            w1_codes[a, b] = kept([P, PASS], U32, f"w1_codes{a}{b}")
            w1_sc[a, b] = kept([P, PASS], U8, f"w1_sc{a}{b}")
            nc.vector.quantize_mx(
                out=w1_codes[a, b][:].bitcast(FP8X4), scales=w1_sc[a, b][:],
                in_=grouped[:].rearrange("p t m i -> p (t m i)"),
            )

        v_codes = [kept([P, S], U32, f"v_codes{a}") for a in range(2)]
        v_sc = [kept([P, S], U8, f"v_sc{a}") for a in range(2)]

        def gather_tab_words(a):
            nc.vector.tensor_copy(out=v_codes[a][:], in_=tab_w[a][:].bitcast(U32).indirect(list1[:]))

        gather_tab_words(0)
        for a in range(2):
            nc.vector.tensor_copy(out=v_sc[a][:], in_=tab_sc[:, a * T : (a + 1) * T].indirect(list1[:]))

        w4_codes, w4_sc = [], []

        def deal_w4_scales(b):
            w4_sc.append(kept([P, 2, PASS], U8, f"w4_sc{b}"))
            nc.vector.tensor_copy(
                out=w4_sc[b][:].rearrange("p a (t m) -> p a t m", t=PACK),
                in_=w4_sc_raw[:].rearrange("p (a b m t) -> p b a t m", a=2, b=2, t=PACK)[:, b],
            )

        def deal_w4_words(b):
            w4_codes.append(kept([P, 2, 2 * PASS], U8, f"w4_codes{b}"))
            nc.scalar.copy(
                out=w4_codes[b][:].bitcast(U16).rearrange("p a (t m) -> p a t m", t=PACK),
                in_=w4_raw[b][:].bitcast(U16).rearrange("p a (m t) -> p a t m", t=PACK),
            )

        quantise_w1(0, 0)
        u_sc_flat = in_place_of("w1_grouped00", [P, S2], U8, "u_sc_flat")
        nc.vector.tensor_copy(out=u_sc_flat[:], in_=tab2_sc[:].indirect(list2[:]))
        deal_w4_words(0)
        deal_w4_scales(0)
        deal_w4_scales(1)
        gather_tab_words(1)
        quantise_w1(1, 0)
        deal_w4_words(1)

        def interleave(copy, dst, src):
            copy(
                out=dst.rearrange("p (c i) t -> p c t i", i=RUN),
                in_=src.rearrange("p t (c i) -> p c t i", i=RUN),
            )

        def w4_pass(acc, a, b, t, start):
            nc.tensor.matmul_mx(
                out=acc[:], lhsT=w4_codes[b][:, a, 2 * t * P : 2 * (t + 1) * P].bitcast(FP4X4),
                lhsT_scale=w4_sc[b][:, a, t * P : (t + 1) * P],
                rhs=v_codes[a][:].bitcast(FP8X4), rhs_scale=v_sc[a][:], start=start, stop=False,
            )

        def w1_pass(acc, a, b, t, start, stop):
            nc.tensor.matmul_mx(
                out=acc[:], lhsT=w1_codes[a, b][:, t * P : (t + 1) * P].bitcast(FP8X4),
                lhsT_scale=w1_sc[a, b][:, t * P : (t + 1) * P],
                rhs=v_codes[a][:].bitcast(FP8X4), rhs_scale=v_sc[a][:], start=start, stop=stop,
            )

        def swish(acc, flat, b, t):
            gate = in_place_of(f"gate{b}{t}", [P, S], F32, "gate")
            nc.scalar.activation(out=gate[:], in_=acc[:], func=ACT.Relu, bias=knee_c[:, b, t : t + 1])
            nc.vector.scalar_tensor_tensor(
                out=flat[:, t, :], in0=gate[:], scalar=roof_c[:, b, t : t + 1], in1=acc[:],
                op0=ALU.min, op1=ALU.mult,
            )

        h_codes, h_sc = [], []

        def quantise_h(flat, b):
            grouped = in_place_of(f"h_grouped{b}", [P, S, PACK], BF16, "h_grouped")
            interleave(nc.scalar.copy, grouped[:], flat[:])
            h_codes.append(kept([P, S], U32, f"h_codes{b}"))
            h_sc.append(kept([P, S], U8, f"h_sc{b}"))
            nc.vector.quantize_mx(
                out=h_codes[b][:].bitcast(FP8X4), scales=h_sc[b][:],
                in_=grouped[:].rearrange("p c t -> p (c t)"),
            )

        accs = [bank(t) for t in range(PACK)]
        for t in range(PACK):
            w1_pass(accs[t], 0, 0, t, True, False)
        for a in range(2):
            for t in range(PACK):
                w4_pass(accs[t], a, 0, t, False)
        quantise_w1(0, 1)
        quantise_w1(1, 1)
        flat0 = work.tile([P, PACK, S], BF16, name="h_flat", align_bytes=64)
        for t in range(PACK):
            w1_pass(accs[t], 1, 0, t, False, True)
            swish(accs[t], flat0, 0, t)

        accs = [bank(PACK + t) for t in range(PACK)]
        for a in range(2):
            for t in range(PACK):
                w4_pass(accs[t], a, 1, t, a == 0)
        for t in range(PACK):
            w1_pass(accs[t], 0, 1, t, False, False)
        flat1 = work.tile([P, PACK, S], BF16, name="h_flat", align_bytes=64)
        for t in range(PACK):
            w1_pass(accs[t], 1, 1, t, False, True)
            swish(accs[t], flat1, 1, t)
        quantise_h(flat0, 0)
        quantise_h(flat1, 1)

        u_sc = in_place_of("w1_grouped10", [P, S2], U8, "u_sc")
        nc.vector.tensor_copy(
            out=u_sc[:].rearrange("p (g t m) -> p g t m", g=2, t=PACK),
            in_=u_sc_flat[:].rearrange("p (g m t) -> p g t m", g=2, t=PACK),
        )

        u_codes = {}

        def gather_tab2_words(a, g, tag):
            u_codes[a, g] = in_place_of(tag, [P, PASS], U32, "u_codes")
            entries = list2[:, g * PASS // LIST_ROWS : (g + 1) * PASS // LIST_ROWS]
            nc.vector.tensor_copy(
                out=u_codes[a, g][:].rearrange("p (t m) -> p m t", t=PACK),
                in_=tab2_w[a][:].bitcast(U32).indirect(entries),
            )

        gather_tab2_words(0, 0, "gate11")
        gather_tab2_words(0, 1, "gate12")
        gather_tab2_words(1, 0, "h_grouped0")
        gather_tab2_words(1, 1, "h_grouped1")

        def strength_pass(acc, a, g, t):
            col = g * PASS + t * P
            nc.tensor.matmul_mx(
                out=acc[:], lhsT=u_codes[a, g][:, t * P : (t + 1) * P].bitcast(FP8X4),
                lhsT_scale=u_sc[TAB2_ROW + 4 * a : P, col : col + P],
                rhs=h_codes[a][:].bitcast(FP8X4), rhs_scale=h_sc[a][:],
                start=(a == 0), stop=(a == 1),
            )

        y_sc = kept([P, 2, S], U8, "y_sc")
        out_rows = out_0.rearrange("(g p t) j -> g p t j", g=2, t=PACK)
        y, y_grouped = [], []

        def strengths(acc, g, t):
            strength_pass(acc, 1, g, t)
            above = work.tile([P, S], F32, name="above", bufs=PACK, align_bytes=64)
            nc.scalar.activation(out=above[:], in_=acc[:], func=ACT.Relu, bias=bias_c[:, g, t : t + 1])
            nc.vector.tensor_scalar(
                out=y[g][:, t, :], in0=above[:], scalar1=top_c[:, g, t : t + 1], scalar2=None, op0=ALU.min,
            )
            if t % 2 == 1:
                nc.sync.dma_start(out=out_rows[g, :, t - 1 : t + 1, :], in_=y[g][:, t - 1 : t + 1, :])

        def new_y():
            y.append(work.tile([P, PACK, S], F32, name="y", align_bytes=64))
            y_grouped.append(work.tile([P, S, PACK], BF16, name="y_grouped", align_bytes=64))

        accs = [bank(t) for t in range(PACK)]
        for t in range(PACK):
            strength_pass(accs[t], 0, 0, t)
        new_y()
        for t in range(PACK):
            strengths(accs[t], 0, t)
        new_y()
        for t in range(PACK):
            acc = bank(t)
            strength_pass(acc, 0, 1, t)
            strengths(acc, 1, t)

        def round_y(copy, g, cols):
            interleave(copy, y_grouped[g][:, cols, :], y[g][:, :, cols])

        def quantise_y(g, cols, codes):
            nc.vector.quantize_mx(
                out=codes[:, cols].bitcast(FP8X4), scales=y_sc[:, g, cols],
                in_=y_grouped[g][:, cols, :].rearrange("p c t -> p (c t)"),
            )
            words = out_1[g].rearrange("p m t -> p (m t)").bitcast(I32)
            nc.sync.dma_start(out=words[:, cols], in_=codes[:, cols])

        left, right = slice(0, S // 2), slice(S // 2, S)
        round_y(nc.vector.tensor_copy, 0, left)
        round_y(nc.vector.tensor_copy, 0, right)
        round_y(nc.scalar.copy, 1, left)
        round_y(nc.vector.tensor_copy, 1, right)
        quantise_y(0, slice(0, S), kept([P, S], I32, "y_codes0"))
        y_codes1 = kept([P, S], I32, "y_codes1")
        quantise_y(1, right, y_codes1)
        quantise_y(1, left, y_codes1)
        for q in range(QUADS):
            nc.scalar.dma_start(
                out=out_2[:, 4 * q : 4 * q + 4, :].bitcast(I32).rearrange("g r n -> r g n"),
                in_=y_sc[QUAD * q : QUAD * q + 4, :, :].bitcast(I32),
            )
